import numpy as np, ml_dtypes
CORES = [78,86,94,102,110,118]
N = 6
NP, TK = 3, 512
def setup_inputs(rng):
    return {"x": rng.standard_normal((N, 128, TK), dtype=np.float32).astype(ml_dtypes.bfloat16), "w1": (rng.standard_normal((N, 128, 128), dtype=np.float32) / 8).astype(ml_dtypes.bfloat16), "w2": (rng.standard_normal((N, 128, NP * 128), dtype=np.float32) / 8).astype(ml_dtypes.bfloat16)}
def setup_inputs_big(rng):
    d = setup_inputs(rng)
    for k in ("x", "w1", "w2"): d[k] = (d[k].astype(np.float32) * 1024.0).astype(d[k].dtype)
    return d
def setup_inputs_small(rng):
    d = setup_inputs(rng)
    for k in ("x", "w1", "w2"): d[k] = (d[k].astype(np.float32) * (1 / 1024.0)).astype(d[k].dtype)
    return d
def setup_inputs_apart(rng):
    d = setup_inputs(rng)
    f = (10.0 ** rng.permutation(np.linspace(-1.5, 1.5, N))).astype(np.float32).reshape(N, 1, 1)
    for k in ("x", "w1", "w2"): d[k] = (d[k].astype(np.float32) * f).astype(d[k].dtype)
    return d
def reference(x, w1, w2):
    X, W1, W2 = x.astype(np.float64), w1.astype(np.float64), w2.astype(np.float64)
    h = [np.maximum(W1[p].T @ X[p], 0.0) for p in range(NP)]
    y = np.full((N, 128, TK), np.nan)
    for q in range(NP, N):
        y[q] = sum(W2[q][:, 128 * p:128 * p + 128].T @ h[p] for p in range(NP))
    return {"y": y.astype(ml_dtypes.bfloat16 if x.dtype != np.float64 else np.float64)}

@@ -1,0 +1,83 @@
+from concourse.bass import DstId, RemoteDMATransfer
+from concourse.mybir import AluOpType
+
+NP = 3
+TK = 512
+HF = TK // 2
+
+SCRATCH = {
+    "xs": ("sbuf", [128, TK], "bfloat16"),
+    "w1s": ("sbuf", [128, 128], "bfloat16"),
+    "w2s": ("sbuf", [128, NP * 128], "bfloat16"),
+    "zero": ("sbuf", [128, HF], "bfloat16"),
+    "h": ("sbuf", [128, TK], "bfloat16"),
+    "h0": ("sbuf", [128, TK], "bfloat16"),
+    "h1": ("sbuf", [128, TK], "bfloat16"),
+    "h2": ("sbuf", [128, TK], "bfloat16"),
+    "ys": ("sbuf", [128, TK], "bfloat16"),
+    "psA": ("psum", [128, 512], "float32"),
+    "psB": ("psum", [128, 512], "float32"),
+}
+SEMAPHORES = ["ld", "fill", "mmA", "mmB", "vA", "vB", "sent", "arr0", "arr1", "arr2", "st"]
+
+
+def bits(mask):
+    return bin(mask).count("1")
+
+
+def rank_program(g, core, T, topo):
+    rank = T.rank_of(core)
+    if rank is None:
+        return
+    S = T.sem
+    halves = ((T.psA, S.mmA, S.vA, 0), (T.psB, S.mmB, S.vB, HF))
+
+    if rank < NP:
+        p = rank
+        g.sync.dma_start(T.xs[:], T.x[:]).then_inc(S.ld, 16)
+        g.scalar.dma_start(T.w1s[:], T.w1[:]).then_inc(S.ld, 16)
+        g.vector.memset(T.zero[:], 0.0).then_inc(S.fill, 1)
+        g.tensor.wait_ge(S.ld, 32)
+        for ps, mm, _, c0 in halves:
+            g.tensor.matmul(ps[:, 0:HF], T.w1s[:], T.xs[:, c0:c0 + HF], True, True).then_inc(mm, 1)
+        g.vector.wait_ge(S.fill, 1)
+        for ps, mm, v, c0 in halves:
+            g.vector.wait_ge(mm, 1)
+            g.vector.tensor_tensor(T.h[:, c0:c0 + HF], ps[:, 0:HF], T.zero[:], AluOpType.max).then_inc(v, 1)
+        dsts = [T.cores[NP + (p + k) % NP] for k in (0, 2, 1)]
+        mask = topo.mask(core, dsts[0])
+        for d in dsts:
+            mask &= topo.mask(core, d)
+        ids = []
+        for d in dsts:
+            rid, pid, _ = topo.addr(d)
+            ids.append(DstId(rid=rid, pnc=pid))
+        land = T["h%d" % p]
+        g.wait_ge(S.vA, 1)
+        g.wait_ge(S.vB, 1)
+        g.remote_dma_fused(
+            [RemoteDMATransfer(dst_ids=ids, dma_engine_mask=mask, remote_sem=S["arr%d" % p],
+                               srcs=[T.h[:]], dsts=[land[:] for _ in dsts])],
+            local_sem=S.sent)
+        g.wait_ge(S.sent, bits(mask))
+        return
+
+    j = rank - NP
+    g.sync.dma_start(T.w2s[:], T.w2[:]).then_inc(S.ld, 16)
+    g.tensor.wait_ge(S.ld, 16)
+    order = [(j + k) % NP for k in range(NP)]
+    for n, p in enumerate(order):
+        src = T.cores[p]
+        g.tensor.wait_ge(S["arr%d" % p], bits(topo.mask(src, core)))
+        for ps, mm, _, c0 in halves:
+            i = g.tensor.matmul(ps[:, 0:HF], T.w2s[:, 128 * p:128 * p + 128], T["h%d" % p][:, c0:c0 + HF],
+                                n == 0, n == NP - 1)
+            if n == NP - 1:
+                i.then_inc(mm, 1)
+    for ps, mm, v, c0 in halves:
+        g.vector.wait_ge(mm, 1)
+        g.vector.tensor_copy(T.ys[:, c0:c0 + HF], ps[:, 0:HF]).then_inc(v, 1)
+    g.sync.wait_ge(S.vA, 1)
+    g.sync.wait_ge(S.vB, 1)
+    g.sync.dma_start(T.y[:], T.ys[:]).then_inc(S.st, 16)
+    g.sync.wait_ge(S.st, 16)

@@ -3,26 +3,37 @@ from concourse.mybir import AluOpType
 
 NP = 3
 TK = 512
-HF = TK // 2
+CUTS = [0, 256, 512]
+NB = len(CUTS) - 1
+WMAX = max(CUTS[b + 1] - CUTS[b] for b in range(NB))
 
 SCRATCH = {
     "xs": ("sbuf", [128, TK], "bfloat16"),
     "w1s": ("sbuf", [128, 128], "bfloat16"),
     "w2s": ("sbuf", [128, NP * 128], "bfloat16"),
-    "zero": ("sbuf", [128, HF], "bfloat16"),
+    "zero": ("sbuf", [128, WMAX], "bfloat16"),
     "h": ("sbuf", [128, TK], "bfloat16"),
     "h0": ("sbuf", [128, TK], "bfloat16"),
     "h1": ("sbuf", [128, TK], "bfloat16"),
     "h2": ("sbuf", [128, TK], "bfloat16"),
     "ys": ("sbuf", [128, TK], "bfloat16"),
-    "psA": ("psum", [128, 512], "float32"),
-    "psB": ("psum", [128, 512], "float32"),
 }
-SEMAPHORES = ["ld", "fill", "mmA", "mmB", "vA", "vB", "sent", "arr0", "arr1", "arr2", "st"]
+SEMAPHORES = ["ldw", "fill", "sent"]
+for _b in range(NB):
+    SCRATCH["ps%d" % _b] = ("psum", [128, 512], "float32")
+    SEMAPHORES += ["ld%d" % _b, "mm%d" % _b, "v%d" % _b, "st%d" % _b]
+    SEMAPHORES += ["arr%d_%d" % (_p, _b) for _p in range(NP)]
 
 
 def bits(mask):
     return bin(mask).count("1")
+
+
+def common_mask(topo, src, dsts):
+    mask = topo.mask(src, dsts[0])
+    for d in dsts:
+        mask &= topo.mask(src, d)
+    return mask
 
 
 def rank_program(g, core, T, topo):
@@ -30,54 +41,55 @@ def rank_program(g, core, T, topo):
     if rank is None:
         return
     S = T.sem
-    halves = ((T.psA, S.mmA, S.vA, 0), (T.psB, S.mmB, S.vB, HF))
+    qs = list(T.cores[NP:])
+    blocks = [(b, CUTS[b], CUTS[b + 1]) for b in range(NB)]
 
     if rank < NP:
         p = rank
-        g.sync.dma_start(T.xs[:], T.x[:]).then_inc(S.ld, 16)
-        g.scalar.dma_start(T.w1s[:], T.w1[:]).then_inc(S.ld, 16)
+        g.scalar.dma_start(T.w1s[:], T.w1[:]).then_inc(S.ldw, 16)
+        for b, lo, hi in blocks:
+            g.sync.dma_start(T.xs[:, lo:hi], T.x[:, lo:hi]).then_inc(S["ld%d" % b], 16)
         g.vector.memset(T.zero[:], 0.0).then_inc(S.fill, 1)
-        g.tensor.wait_ge(S.ld, 32)
-        for ps, mm, _, c0 in halves:
-            g.tensor.matmul(ps[:, 0:HF], T.w1s[:], T.xs[:, c0:c0 + HF], True, True).then_inc(mm, 1)
+        g.tensor.wait_ge(S.ldw, 16)
+        for b, lo, hi in blocks:
+            g.tensor.wait_ge(S["ld%d" % b], 16)
+            g.tensor.matmul(T["ps%d" % b][:, 0:hi - lo], T.w1s[:], T.xs[:, lo:hi], True, True).then_inc(S["mm%d" % b], 1)
         g.vector.wait_ge(S.fill, 1)
-        for ps, mm, v, c0 in halves:
-            g.vector.wait_ge(mm, 1)
-            g.vector.tensor_tensor(T.h[:, c0:c0 + HF], ps[:, 0:HF], T.zero[:], AluOpType.max).then_inc(v, 1)
-        dsts = [T.cores[NP + (p + k) % NP] for k in (0, 2, 1)]
-        mask = topo.mask(core, dsts[0])
-        for d in dsts:
-            mask &= topo.mask(core, d)
+        for b, lo, hi in blocks:
+            g.vector.wait_ge(S["mm%d" % b], 1)
+            g.vector.tensor_tensor(T.h[:, lo:hi], T["ps%d" % b][:, 0:hi - lo], T.zero[:, 0:hi - lo],
+                                   AluOpType.max).then_inc(S["v%d" % b], 1)
+        dsts = [qs[(p + k) % NP] for k in (0, 2, 1)]
+        mask = common_mask(topo, core, qs)
         ids = []
         for d in dsts:
             rid, pid, _ = topo.addr(d)
             ids.append(DstId(rid=rid, pnc=pid))
-        land = T["h%d" % p]
-        g.wait_ge(S.vA, 1)
-        g.wait_ge(S.vB, 1)
-        g.remote_dma_fused(
-            [RemoteDMATransfer(dst_ids=ids, dma_engine_mask=mask, remote_sem=S["arr%d" % p],
-                               srcs=[T.h[:]], dsts=[land[:] for _ in dsts])],
-            local_sem=S.sent)
-        g.wait_ge(S.sent, bits(mask))
+        for b, lo, hi in blocks:
+            g.wait_ge(S["v%d" % b], 1)
+            g.remote_dma_fused(
+                [RemoteDMATransfer(dst_ids=ids, dma_engine_mask=mask, remote_sem=S["arr%d_%d" % (p, b)],
+                                   srcs=[T.h[:, lo:hi]], dsts=[T["h%d" % p][:, lo:hi] for _ in dsts])],
+                local_sem=S.sent)
+        g.wait_ge(S.sent, NB * bits(mask))
         return
 
     j = rank - NP
-    g.sync.dma_start(T.w2s[:], T.w2[:]).then_inc(S.ld, 16)
-    g.tensor.wait_ge(S.ld, 16)
+    g.sync.dma_start(T.w2s[:], T.w2[:]).then_inc(S.ldw, 16)
+    g.tensor.wait_ge(S.ldw, 16)
     order = [(j + k) % NP for k in range(NP)]
-    for n, p in enumerate(order):
-        src = T.cores[p]
-        g.tensor.wait_ge(S["arr%d" % p], bits(topo.mask(src, core)))
-        for ps, mm, _, c0 in halves:
-            i = g.tensor.matmul(ps[:, 0:HF], T.w2s[:, 128 * p:128 * p + 128], T["h%d" % p][:, c0:c0 + HF],
+    for b, lo, hi in blocks:
+        for n, p in enumerate(order):
+            g.tensor.wait_ge(S["arr%d_%d" % (p, b)], bits(common_mask(topo, T.cores[p], qs)))
+            i = g.tensor.matmul(T["ps%d" % b][:, 0:hi - lo], T.w2s[:, 128 * p:128 * p + 128], T["h%d" % p][:, lo:hi],
                                 n == 0, n == NP - 1)
             if n == NP - 1:
-                i.then_inc(mm, 1)
-    for ps, mm, v, c0 in halves:
-        g.vector.wait_ge(mm, 1)
-        g.vector.tensor_copy(T.ys[:, c0:c0 + HF], ps[:, 0:HF]).then_inc(v, 1)
-    g.sync.wait_ge(S.vA, 1)
-    g.sync.wait_ge(S.vB, 1)
-    g.sync.dma_start(T.y[:], T.ys[:]).then_inc(S.st, 16)
-    g.sync.wait_ge(S.st, 16)
+                i.then_inc(S["mm%d" % b], 1)
+    for b, lo, hi in blocks:
+        g.vector.wait_ge(S["mm%d" % b], 1)
+        g.vector.tensor_copy(T.ys[:, lo:hi], T["ps%d" % b][:, 0:hi - lo]).then_inc(S["v%d" % b], 1)
+    for b, lo, hi in blocks:
+        q = g.sync if b % 2 == 0 else g.scalar
+        q.wait_ge(S["v%d" % b], 1)
+        q.dma_start(T.y[:, lo:hi], T.ys[:, lo:hi]).then_inc(S["st%d" % b], 16)
+        q.wait_ge(S["st%d" % b], 16)

@@ -1,28 +1,32 @@
 from concourse.bass import DstId, RemoteDMATransfer
-from concourse.mybir import AluOpType
+from concourse.mybir import AluOpType, ActivationFunctionType
 
 NP = 3
 TK = 512
-CUTS = [0, 256, 512]
-NB = len(CUTS) - 1
-WMAX = max(CUTS[b + 1] - CUTS[b] for b in range(NB))
+NR, WR = 2, 48
+WC2 = 128
+D0 = NR * WR
+PIECE = {"R": (0, D0), "D": (D0, TK), "C1": (D0, TK - WC2), "C2": (TK - WC2, TK)}
+for _i in range(NR):
+    PIECE["R%d" % _i] = (_i * WR, (_i + 1) * WR)
 
 SCRATCH = {
     "xs": ("sbuf", [128, TK], "bfloat16"),
     "w1s": ("sbuf", [128, 128], "bfloat16"),
     "w2s": ("sbuf", [128, NP * 128], "bfloat16"),
-    "zero": ("sbuf", [128, WMAX], "bfloat16"),
+    "zero": ("sbuf", [128, max(D0, WC2)], "bfloat16"),
     "h": ("sbuf", [128, TK], "bfloat16"),
     "h0": ("sbuf", [128, TK], "bfloat16"),
     "h1": ("sbuf", [128, TK], "bfloat16"),
     "h2": ("sbuf", [128, TK], "bfloat16"),
     "ys": ("sbuf", [128, TK], "bfloat16"),
 }
-SEMAPHORES = ["ldw", "fill", "sent"]
-for _b in range(NB):
-    SCRATCH["ps%d" % _b] = ("psum", [128, 512], "float32")
-    SEMAPHORES += ["ld%d" % _b, "mm%d" % _b, "v%d" % _b, "st%d" % _b]
-    SEMAPHORES += ["arr%d_%d" % (_p, _b) for _p in range(NP)]
+SEMAPHORES = ["ldw", "ldR", "ldD", "fill", "sent", "hand"]
+for _k in ("R", "C1", "C2"):
+    SCRATCH["ps" + _k] = ("psum", [128, 512], "float32")
+    SEMAPHORES += ["mm" + _k, "v" + _k, "st" + _k]
+for _p in range(NP):
+    SEMAPHORES += ["arr%s_%d" % (_k, _p) for _k in ("D", "C1", "C2", "R0", "R1")]
 
 
 def bits(mask):
@@ -36,60 +40,132 @@ def common_mask(topo, src, dsts):
     return mask
 
 
+def relays_of(topo, core, qs, n_cores):
+    c = [k for k in range(n_cores) if k != core and topo.chip(k) == topo.chip(core)
+         and all(topo.may_write(k, q) for q in qs)]
+    c.sort(key=lambda k: (topo.die(k) == topo.die(core), k))
+    return c[:NR]
+
+
+def ids_of(topo, cores):
+    out = []
+    for d in cores:
+        rid, pid, _ = topo.addr(d)
+        out.append(DstId(rid=rid, pnc=pid))
+    return out
+
+
+def hand_masks(topo, core, relays, qs):
+    free = common_mask(topo, core, relays) & ~common_mask(topo, core, qs)
+    on = [i for i in range(16) if (free >> i) & 1]
+    n = len(on) // NR
+    return [sum(1 << i for i in on[r * n:(r + 1) * n]) for r in range(NR)]
+
+
 def rank_program(g, core, T, topo):
-    rank = T.rank_of(core)
-    if rank is None:
-        return
     S = T.sem
-    qs = list(T.cores[NP:])
-    blocks = [(b, CUTS[b], CUTS[b + 1]) for b in range(NB)]
+    ps, qs = list(T.cores[:NP]), list(T.cores[NP:])
+    n_cores = topo.CHIPS * topo.CORES_PER_CHIP
+    role = [(p, (p + 2) % NP, (p + 1) % NP) for p in range(NP)]
+    relays = [relays_of(topo, c, qs, n_cores) for c in ps]
+    rank = T.rank_of(core)
+
+    def cols(t, k):
+        return t[:, PIECE[k][0]:PIECE[k][1]]
+
+    def bank(k):
+        return T["ps" + k][:, 0:PIECE[k][1] - PIECE[k][0]]
+
+    def send(k, p, to, mask):
+        g.remote_dma_fused(
+            [RemoteDMATransfer(dst_ids=ids_of(topo, [qs[i] for i in to]), dma_engine_mask=mask,
+                               remote_sem=S["arr%s_%d" % (k, p)],
+                               srcs=[cols(T.h, k)], dsts=[cols(T["h%d" % p], k) for _ in to])],
+            local_sem=S.sent)
+
+    if rank is None:
+        for p in range(NP):
+            for r, c in enumerate(relays[p]):
+                if c == core:
+                    mask = common_mask(topo, core, qs)
+                    g.wait_ge(S.hand, bits(hand_masks(topo, ps[p], relays[p], qs)[r]))
+                    send("R%d" % r, p, [role[p][(r + 1 + n) % NP] for n in range(NP)], mask)
+                    g.wait_ge(S.sent, bits(mask))
+        return
 
     if rank < NP:
         p = rank
         g.scalar.dma_start(T.w1s[:], T.w1[:]).then_inc(S.ldw, 16)
-        for b, lo, hi in blocks:
-            g.sync.dma_start(T.xs[:, lo:hi], T.x[:, lo:hi]).then_inc(S["ld%d" % b], 16)
+        g.sync.dma_start(cols(T.xs, "R"), cols(T.x, "R")).then_inc(S.ldR, 16)
+        g.sync.dma_start(cols(T.xs, "D"), cols(T.x, "D")).then_inc(S.ldD, 16)
         g.vector.memset(T.zero[:], 0.0).then_inc(S.fill, 1)
         g.tensor.wait_ge(S.ldw, 16)
-        for b, lo, hi in blocks:
-            g.tensor.wait_ge(S["ld%d" % b], 16)
-            g.tensor.matmul(T["ps%d" % b][:, 0:hi - lo], T.w1s[:], T.xs[:, lo:hi], True, True).then_inc(S["mm%d" % b], 1)
+        g.tensor.wait_ge(S.ldR, 16)
+        g.tensor.matmul(bank("R"), T.w1s[:], cols(T.xs, "R"), True, True).then_inc(S.mmR, 1)
+        g.tensor.wait_ge(S.ldD, 16)
+        for k in ("C1", "C2"):
+            g.tensor.matmul(bank(k), T.w1s[:], cols(T.xs, k), True, True).then_inc(S["mm" + k], 1)
         g.vector.wait_ge(S.fill, 1)
-        for b, lo, hi in blocks:
-            g.vector.wait_ge(S["mm%d" % b], 1)
-            g.vector.tensor_tensor(T.h[:, lo:hi], T["ps%d" % b][:, 0:hi - lo], T.zero[:, 0:hi - lo],
-                                   AluOpType.max).then_inc(S["v%d" % b], 1)
-        dsts = [qs[(p + k) % NP] for k in (0, 2, 1)]
+        for k in ("R", "C2"):
+            g.vector.wait_ge(S["mm" + k], 1)
+            g.vector.tensor_tensor(cols(T.h, k), bank(k), T.zero[:, 0:PIECE[k][1] - PIECE[k][0]],
+                                   AluOpType.max).then_inc(S["v" + k], 1)
+        g.scalar.wait_ge(S.mmC1, 1)
+        g.scalar.activation(cols(T.h, "C1"), bank("C1"), ActivationFunctionType.Relu).then_inc(S.vC1, 1)
+        x, y, z = role[p]
         mask = common_mask(topo, core, qs)
-        ids = []
-        for d in dsts:
-            rid, pid, _ = topo.addr(d)
-            ids.append(DstId(rid=rid, pnc=pid))
-        for b, lo, hi in blocks:
-            g.wait_ge(S["v%d" % b], 1)
-            g.remote_dma_fused(
-                [RemoteDMATransfer(dst_ids=ids, dma_engine_mask=mask, remote_sem=S["arr%d_%d" % (p, b)],
-                                   srcs=[T.h[:, lo:hi]], dsts=[T["h%d" % p][:, lo:hi] for _ in dsts])],
-                local_sem=S.sent)
-        g.wait_ge(S.sent, NB * bits(mask))
+        hm = hand_masks(topo, core, relays[p], qs)
+        g.wait_ge(S.vR, 1)
+        g.remote_dma_fused(
+            [RemoteDMATransfer(dst_ids=ids_of(topo, [relays[p][r]]), dma_engine_mask=hm[r], remote_sem=S.hand,
+                               srcs=[cols(T.h, "R%d" % r)], dsts=[cols(T.h, "R%d" % r)]) for r in range(NR)],
+            local_sem=S.sent)
+        g.wait_ge(S.vC1, 1)
+        g.wait_ge(S.vC2, 1)
+        send("D", p, [x, y], mask)
+        send("C1", p, [z], mask)
+        send("C2", p, [z], mask)
+        g.wait_ge(S.sent, 3 * bits(mask) + sum(bits(m) for m in hm))
         return
 
     j = rank - NP
+    a = [p for p in range(NP) if role[p][0] == j][0]
+    b = [p for p in range(NP) if role[p][1] == j][0]
+    c = [p for p in range(NP) if role[p][2] == j][0]
+
+    def arrived(k, p, src):
+        g.tensor.wait_ge(S["arr%s_%d" % (k, p)], bits(common_mask(topo, src, qs)))
+
+    def mm(k, p, start, stop):
+        i = g.tensor.matmul(bank(k), T.w2s[:, 128 * p:128 * p + 128], cols(T["h%d" % p], k), start, stop)
+        if stop:
+            i.then_inc(S["mm" + k], 1)
+
     g.sync.dma_start(T.w2s[:], T.w2[:]).then_inc(S.ldw, 16)
     g.tensor.wait_ge(S.ldw, 16)
-    order = [(j + k) % NP for k in range(NP)]
-    for b, lo, hi in blocks:
-        for n, p in enumerate(order):
-            g.tensor.wait_ge(S["arr%d_%d" % (p, b)], bits(common_mask(topo, T.cores[p], qs)))
-            i = g.tensor.matmul(T["ps%d" % b][:, 0:hi - lo], T.w2s[:, 128 * p:128 * p + 128], T["h%d" % p][:, lo:hi],
-                                n == 0, n == NP - 1)
-            if n == NP - 1:
-                i.then_inc(S["mm%d" % b], 1)
-    for b, lo, hi in blocks:
-        g.vector.wait_ge(S["mm%d" % b], 1)
-        g.vector.tensor_copy(T.ys[:, lo:hi], T["ps%d" % b][:, 0:hi - lo]).then_inc(S["v%d" % b], 1)
-    for b, lo, hi in blocks:
-        q = g.sync if b % 2 == 0 else g.scalar
-        q.wait_ge(S["v%d" % b], 1)
-        q.dma_start(T.y[:, lo:hi], T.ys[:, lo:hi]).then_inc(S["st%d" % b], 16)
-        q.wait_ge(S["st%d" % b], 16)
+    arrived("D", a, ps[a])
+    mm("C1", a, True, False)
+    mm("C2", a, True, False)
+    arrived("D", b, ps[b])
+    mm("C1", b, False, False)
+    mm("C2", b, False, False)
+    arrived("C1", c, ps[c])
+    mm("C1", c, False, True)
+    for n, p in enumerate((c, a, b)):
+        for r in range(NR):
+            arrived("R%d" % r, p, relays[p][r])
+        mm("R", p, n == 0, n == NP - 1)
+    arrived("C2", c, ps[c])
+    mm("C2", c, False, True)
+    g.scalar.wait_ge(S.mmC1, 1)
+    g.scalar.activation(cols(T.ys, "C1"), bank("C1"), ActivationFunctionType.Copy).then_inc(S.vC1, 1)
+    g.scalar.wait_ge(S.vC1, 1)
+    g.scalar.dma_start(cols(T.y, "C1"), cols(T.ys, "C1")).then_inc(S.stC1, 16)
+    for k in ("R", "C2"):
+        g.vector.wait_ge(S["mm" + k], 1)
+        g.vector.tensor_copy(cols(T.ys, k), bank(k)).then_inc(S["v" + k], 1)
+        g.sync.wait_ge(S["v" + k], 1)
+        g.sync.dma_start(cols(T.y, k), cols(T.ys, k)).then_inc(S["st" + k], 16)
+    g.sync.wait_ge(S.stR, 16)
+    g.sync.wait_ge(S.stC2, 16)
+    g.scalar.wait_ge(S.stC1, 16)

from concourse.bass import DstId, RemoteDMATransfer
from concourse.mybir import AluOpType, ActivationFunctionType

NP = 3
TK = 512
NR, WR = 2, 48
WC2 = 128
D0 = NR * WR
PIECE = {"R": (0, D0), "D": (D0, TK), "C1": (D0, TK - WC2), "C2": (TK - WC2, TK)}
for _i in range(NR):
    PIECE["R%d" % _i] = (_i * WR, (_i + 1) * WR)

SCRATCH = {
    "xs": ("sbuf", [128, TK], "bfloat16"),
    "w1s": ("sbuf", [128, 128], "bfloat16"),
    "w2s": ("sbuf", [128, NP * 128], "bfloat16"),
    "zero": ("sbuf", [128, max(D0, WC2)], "bfloat16"),
    "h": ("sbuf", [128, TK], "bfloat16"),
    "h0": ("sbuf", [128, TK], "bfloat16"),
    "h1": ("sbuf", [128, TK], "bfloat16"),
    "h2": ("sbuf", [128, TK], "bfloat16"),
    "ys": ("sbuf", [128, TK], "bfloat16"),
}
SEMAPHORES = ["ldw", "ldR", "ldD", "fill", "sent", "hand"]
for _k in ("R", "C1", "C2"):
    SCRATCH["ps" + _k] = ("psum", [128, 512], "float32")
    SEMAPHORES += ["mm" + _k, "v" + _k, "st" + _k]
for _p in range(NP):
    SEMAPHORES += ["arr%s_%d" % (_k, _p) for _k in ("D", "C1", "C2", "R0", "R1")]


def bits(mask):
    return bin(mask).count("1")


def common_mask(topo, src, dsts):
    mask = topo.mask(src, dsts[0])
    for d in dsts:
        mask &= topo.mask(src, d)
    return mask


def relays_of(topo, core, qs, n_cores):
    c = [k for k in range(n_cores) if k != core and topo.chip(k) == topo.chip(core)
         and all(topo.may_write(k, q) for q in qs)]
    c.sort(key=lambda k: (topo.die(k) == topo.die(core), k))
    return c[:NR]


def ids_of(topo, cores):
    out = []
    for d in cores:
        rid, pid, _ = topo.addr(d)
        out.append(DstId(rid=rid, pnc=pid))
    return out


def hand_masks(topo, core, relays, qs):
    free = common_mask(topo, core, relays) & ~common_mask(topo, core, qs)
    on = [i for i in range(16) if (free >> i) & 1]
    n = len(on) // NR
    return [sum(1 << i for i in on[r * n:(r + 1) * n]) for r in range(NR)]


def rank_program(g, core, T, topo):
    S = T.sem
    ps, qs = list(T.cores[:NP]), list(T.cores[NP:])
    n_cores = topo.CHIPS * topo.CORES_PER_CHIP
    role = [(p, (p + 2) % NP, (p + 1) % NP) for p in range(NP)]
    relays = [relays_of(topo, c, qs, n_cores) for c in ps]
    rank = T.rank_of(core)

    def cols(t, k):
        return t[:, PIECE[k][0]:PIECE[k][1]]

    def bank(k):
        return T["ps" + k][:, 0:PIECE[k][1] - PIECE[k][0]]

    def send(k, p, to, mask):
        g.remote_dma_fused(
            [RemoteDMATransfer(dst_ids=ids_of(topo, [qs[i] for i in to]), dma_engine_mask=mask,
                               remote_sem=S["arr%s_%d" % (k, p)],
                               srcs=[cols(T.h, k)], dsts=[cols(T["h%d" % p], k) for _ in to])],
            local_sem=S.sent)

    if rank is None:
        for p in range(NP):
            for r, c in enumerate(relays[p]):
                if c == core:
                    mask = common_mask(topo, core, qs)
                    g.wait_ge(S.hand, bits(hand_masks(topo, ps[p], relays[p], qs)[r]))
                    send("R%d" % r, p, [role[p][(r + 1 + n) % NP] for n in range(NP)], mask)
                    g.wait_ge(S.sent, bits(mask))
        return

    if rank < NP:
        p = rank
        g.scalar.dma_start(T.w1s[:], T.w1[:]).then_inc(S.ldw, 16)
        g.sync.dma_start(cols(T.xs, "R"), cols(T.x, "R")).then_inc(S.ldR, 16)
        g.sync.dma_start(cols(T.xs, "D"), cols(T.x, "D")).then_inc(S.ldD, 16)
        g.vector.memset(T.zero[:], 0.0).then_inc(S.fill, 1)
        g.tensor.wait_ge(S.ldw, 16)
        g.tensor.wait_ge(S.ldR, 16)
        g.tensor.matmul(bank("R"), T.w1s[:], cols(T.xs, "R"), True, True).then_inc(S.mmR, 1)
        g.tensor.wait_ge(S.ldD, 16)
        for k in ("C1", "C2"):
            g.tensor.matmul(bank(k), T.w1s[:], cols(T.xs, k), True, True).then_inc(S["mm" + k], 1)
        g.vector.wait_ge(S.fill, 1)
        for k in ("R", "C2"):
            g.vector.wait_ge(S["mm" + k], 1)
            g.vector.tensor_tensor(cols(T.h, k), bank(k), T.zero[:, 0:PIECE[k][1] - PIECE[k][0]],
                                   AluOpType.max).then_inc(S["v" + k], 1)
        g.scalar.wait_ge(S.mmC1, 1)
        g.scalar.activation(cols(T.h, "C1"), bank("C1"), ActivationFunctionType.Relu).then_inc(S.vC1, 1)
        x, y, z = role[p]
        mask = common_mask(topo, core, qs)
        hm = hand_masks(topo, core, relays[p], qs)
        g.wait_ge(S.vR, 1)
        g.remote_dma_fused(
            [RemoteDMATransfer(dst_ids=ids_of(topo, [relays[p][r]]), dma_engine_mask=hm[r], remote_sem=S.hand,
                               srcs=[cols(T.h, "R%d" % r)], dsts=[cols(T.h, "R%d" % r)]) for r in range(NR)],
            local_sem=S.sent)
        g.wait_ge(S.vC1, 1)
        g.wait_ge(S.vC2, 1)
        send("D", p, [x, y], mask)
        send("C1", p, [z], mask)
        send("C2", p, [z], mask)
        g.wait_ge(S.sent, 3 * bits(mask) + sum(bits(m) for m in hm))
        return

    j = rank - NP
    a = [p for p in range(NP) if role[p][0] == j][0]
    b = [p for p in range(NP) if role[p][1] == j][0]
    c = [p for p in range(NP) if role[p][2] == j][0]

    def arrived(k, p, src):
        g.tensor.wait_ge(S["arr%s_%d" % (k, p)], bits(common_mask(topo, src, qs)))

    def mm(k, p, start, stop):
        i = g.tensor.matmul(bank(k), T.w2s[:, 128 * p:128 * p + 128], cols(T["h%d" % p], k), start, stop)
        if stop:
            i.then_inc(S["mm" + k], 1)

    g.sync.dma_start(T.w2s[:], T.w2[:]).then_inc(S.ldw, 16)
    g.tensor.wait_ge(S.ldw, 16)
    arrived("D", a, ps[a])
    mm("C1", a, True, False)
    mm("C2", a, True, False)
    arrived("D", b, ps[b])
    mm("C1", b, False, False)
    mm("C2", b, False, False)
    arrived("C1", c, ps[c])
    mm("C1", c, False, True)
    for n, p in enumerate((c, a, b)):
        for r in range(NR):
            arrived("R%d" % r, p, relays[p][r])
        mm("R", p, n == 0, n == NP - 1)
    arrived("C2", c, ps[c])
    mm("C2", c, False, True)
    g.scalar.wait_ge(S.mmC1, 1)
    g.scalar.activation(cols(T.ys, "C1"), bank("C1"), ActivationFunctionType.Copy).then_inc(S.vC1, 1)
    g.scalar.wait_ge(S.vC1, 1)
    g.scalar.dma_start(cols(T.y, "C1"), cols(T.ys, "C1")).then_inc(S.stC1, 16)
    for k in ("R", "C2"):
        g.vector.wait_ge(S["mm" + k], 1)
        g.vector.tensor_copy(cols(T.ys, k), bank(k)).then_inc(S["v" + k], 1)
        g.sync.wait_ge(S["v" + k], 1)
        g.sync.dma_start(cols(T.y, k), cols(T.ys, k)).then_inc(S["st" + k], 16)
    g.sync.wait_ge(S.stR, 16)
    g.sync.wait_ge(S.stC2, 16)
    g.scalar.wait_ge(S.stC1, 16)
